import numpy as np
import ml_dtypes


def mxq(x, axis, fmt="e4m3"):
    dtype, down = {"e4m3": (ml_dtypes.float8_e4m3fn, 7), "e5m2": (ml_dtypes.float8_e5m2, 14)}[fmt]
    v = np.moveaxis(np.asarray(x, np.float32).astype(ml_dtypes.bfloat16).astype(np.float64), axis, -1)
    blocks = v.reshape(v.shape[:-1] + (-1, 32))
    amax = np.abs(blocks).max(-1, keepdims=True)
    byte = np.maximum(np.where(amax > 0, np.frexp(amax)[1] - 1 + 127, 0) - down, 1)
    scale = np.exp2(byte - 127.0)
    codes = (blocks / scale).astype(np.float32).astype(dtype).astype(np.float64)
    return np.moveaxis((codes * scale).reshape(v.shape), -1, axis)


WIDE = False


def mx_kscale(k):
    if not WIDE:
        return np.ones(k)
    levels = np.array([10, -10, 5, -5, 0])
    if k % 512:
        return np.exp2(np.random.permutation(np.resize(levels, k // 32))).repeat(32)
    a = np.empty((k // 512, 16))
    for p in range(k // 512):
        a[p, :8] = np.random.permutation(np.resize(levels, 8))
        for g in range(8):
            far = levels[np.abs(levels - a[p, g]) >= 10]
            a[p, g + 8] = far[np.random.randint(len(far))]
    return np.exp2(a.ravel()).repeat(32)


def f64(x):
    return np.asarray(x).astype(np.float64)


def striped8(idx):
    return np.asarray(idx).reshape(8, -1, 16).transpose(0, 2, 1).reshape(128, -1).astype(np.uint16)


def unstriped8(offs):
    return offs.reshape(8, 16, -1).transpose(0, 2, 1).reshape(8, -1).astype(np.int64)


def pick8(x, idx, run):
    r = np.arange(len(x))
    return x[r[:, None], idx[r % (8 * run) // run]]


E2M1 = np.array([0.0, 0.5, 1.0, 1.5, 2.0, 3.0, 4.0, 6.0, -0.0, -0.5, -1.0, -1.5, -2.0, -3.0, -4.0, -6.0])


def pack_weight(w, fmt):
    k, n = w.shape
    w = f64(np.asarray(w, np.float32).astype(ml_dtypes.bfloat16)).reshape(k // 32, 32, n)
    amax = np.abs(w).max(1)
    if fmt == "e4m3":
        byte = np.frexp(amax)[1] - 1 + 127 - 7
    else:
        mant, ex = np.frexp(amax / 6.0)
        byte = np.where(mant > 0.5, ex, ex - 1) + 127
    byte = np.clip(np.where(amax > 0, byte, 1), 1, 254)
    scaled = (w * np.exp2(127.0 - byte)[:, None, :]).reshape(k, n).astype(np.float32)
    by_word = np.ascontiguousarray(scaled.reshape(k // 512, 128, 4, n).transpose(0, 1, 3, 2))
    if fmt == "e4m3":
        words = by_word.astype(ml_dtypes.float8_e4m3fn).view(np.uint8)
    else:
        c = by_word.astype(ml_dtypes.float4_e2m1fn).view(np.uint8) & 0xF
        words = (c[..., 0::2] | (c[..., 1::2] << 4)).reshape(k // 512, 128, 2 * n)
    return np.ascontiguousarray(words), np.ascontiguousarray(byte.astype(np.uint8).reshape(k // 512, 16, n))


def unpack_weight(words, scales, fmt):
    g, _, n = scales.shape
    words = np.ascontiguousarray(words).reshape(g, 128, n, -1)
    if fmt == "e4m3":
        vals = words.view(ml_dtypes.float8_e4m3fn).astype(np.float64)
    else:
        nib = np.empty((g, 128, n, 4), np.uint8)
        nib[..., 0::2] = words & 0xF
        nib[..., 1::2] = words >> 4
        vals = E2M1[nib]
    vals = vals * np.repeat(np.exp2(scales.astype(np.float64) - 127.0), 8, axis=1)[..., None]
    return vals.transpose(0, 1, 3, 2).reshape(g * 512, n)


D, T, I, Q = 512, 1024, 512, 128


def setup_inputs():
    n = np.random.standard_normal
    idx = np.stack([np.random.permutation(T)[:I] for _ in range(8)])
    idx2 = np.stack([np.random.permutation(T)[:I] for _ in range(8)])
    idx3 = np.stack([np.random.permutation(T)[:I] for _ in range(8)])
    fd = mx_kscale(D)
    keysp = pack_weight(n((D, T)) / fd[:, None], "e4m3")
    return {
        "query": (n((D, Q)) * 0.9 / np.sqrt(D) * fd[:, None]).astype(np.float32),
        "query2": (n((D, Q)) * 0.9 / np.sqrt(D) * fd[:, None]).astype(np.float32),
        "keys_words": keysp[0],
        "keys_scales": keysp[1],
        "lam": (np.random.uniform(0.5, 1.5, (Q, 1))).astype(np.float32),
        "old": (1.0 * n((Q, T))).astype(np.float32),
        "offs": striped8(idx),
        "offs2": striped8(idx2),
        "offs3": striped8(idx3),
    }


def reference(query, query2, keys_words, keys_scales, lam, old, offs, offs2, offs3):
    idx = unstriped8(offs)
    idx2 = unstriped8(offs2)
    idx3 = unstriped8(offs3)
    keysu = unpack_weight(keys_words, keys_scales, "e4m3")
    queryq = mxq(f64(query), 0, "e4m3")
    a = queryq.T @ keysu
    query2q = mxq(f64(query2), 0, "e4m3")
    b = query2q.T @ keysu
    w = pick8(a, idx, 16) + pick8(a, idx2, 16) * np.tanh(pick8(b, idx, 16)) * f64(lam)
    f1 = np.zeros((Q, T))
    f1[np.arange(Q)[:, None], idx3[np.arange(Q) % 128 // 16]] = w
    y = np.maximum(f1, f64(old)) + f64(old) * 0.25
    return y

@@ -1,0 +1,168 @@
+from contextlib import ExitStack
+
+import concourse.mybir as mybir
+
+D, T, I, Q = 512, 1024, 512, 128
+FLOPS = 2 * 2 * D * Q * T
+
+F32 = mybir.dt.float32
+BF16 = mybir.dt.bfloat16
+I32 = mybir.dt.int32
+U32 = mybir.dt.uint32
+U16 = mybir.dt.uint16
+U8 = mybir.dt.uint8
+FP8X4 = mybir.dt.float8_e4m3fn_x4
+ALU = mybir.AluOpType
+ACT = mybir.ActivationFunctionType
+
+P = 128
+PACK = 4
+PIECES = 4
+PIECE = T // PIECES
+HALVES = 2
+HALF = I // HALVES
+GROUP = 16
+
+
+def tile_attend_turnedby_lean_largerput_heads_kernel(
+    tc, query, query2, keys_words, keys_scales, lam, old, offs, offs2, offs3, out
+):
+    nc = tc.nc
+    with ExitStack() as ctx:
+        sb = ctx.enter_context(tc.tile_pool(name="sb", bufs=1))
+        ps = ctx.enter_context(tc.psum_pool(name="ps", bufs=1))
+
+        planes = sb.tile([P, PIECE], U8, name="planes", align_bytes=64)
+        nc.vector.memset(planes[:].bitcast(I32), 0)
+
+        q2_raw = sb.tile([P, PACK, Q], F32, name="q2_raw")
+        q_raw = sb.tile([P, PACK, Q], F32, name="q_raw")
+        key_loads = [(0, 2), (2, 3), (3, 4)]
+        key_tiles = [
+            sb.tile([P, (hi - lo) * PIECE], I32, name=f"key_words{lo}", align_bytes=64) for lo, hi in key_loads
+        ]
+        key_words = [
+            key_tiles[n][:, (j - lo) * PIECE : (j - lo + 1) * PIECE]
+            for n, (lo, hi) in enumerate(key_loads)
+            for j in range(lo, hi)
+        ]
+        words_hbm = keys_words[0].rearrange("p n t -> p (n t)").bitcast(I32)
+        scales_hbm = keys_scales[0].bitcast(I32)
+
+        def load_keys(n):
+            lo, hi = key_loads[n]
+            nc.sync.dma_start(out=key_tiles[n][:], in_=words_hbm[:, lo * PIECE : hi * PIECE])
+
+        nc.sync.dma_start(out=q2_raw[:], in_=query2.rearrange("(p j) m -> p j m", j=PACK))
+        for quad in range(4):
+            nc.scalar.dma_start(
+                out=planes[32 * quad : 32 * quad + 16, :].bitcast(I32),
+                in_=scales_hbm[4 * quad : 4 * quad + 4, :].rearrange("r (j c) -> j r c", j=PIECES),
+            )
+        load_keys(0)
+        nc.sync.dma_start(out=q_raw[:], in_=query.rearrange("(p j) m -> p j m", j=PACK))
+        load_keys(1)
+        load_keys(2)
+        idx = sb.tile([P, I // GROUP], U16, name="idx")
+        idx2 = sb.tile([P, I // GROUP], U16, name="idx2")
+        idx3 = sb.tile([P, I // GROUP], U16, name="idx3")
+        lam_sb = sb.tile([P, 1], F32, name="lam_sb")
+        old_sb = sb.tile([P, T], F32, name="old_sb")
+        nc.sync.dma_start(idx[:], offs)
+        nc.gpsimd.dma_start(out=lam_sb[:], in_=lam)
+        nc.sync.dma_start(idx2[:], offs2)
+        nc.sync.dma_start(idx3[:], offs3)
+        nc.sync.dma_start(out=old_sb[:], in_=old)
+
+        f1 = sb.tile([P, T], F32, name="f1")
+        nc.vector.memset(f1[:], 0.0)
+
+        def quantise(raw, tag):
+            grouped = sb.tile([P, Q, PACK], BF16, name=f"{tag}_grouped", align_bytes=64)
+            nc.vector.tensor_copy(
+                out=grouped[:].rearrange("p (c i) t -> p c t i", i=4),
+                in_=raw[:].rearrange("p t (c i) -> p c t i", i=4),
+            )
+            codes = sb.tile([P, Q], U32, name=f"{tag}_codes", align_bytes=64)
+            scales = sb.tile([P, Q], U8, name=f"{tag}_scales", align_bytes=64)
+            nc.vector.quantize_mx(
+                out=codes[:].bitcast(FP8X4), scales=scales[:], in_=grouped[:].rearrange("p m t -> p (m t)")
+            )
+            return codes, scales
+
+        def score(codes, scales, j, tag):
+            bank = ps.tile([P, PIECE], F32, name=f"{tag}_bank{j}")
+            nc.tensor.matmul_mx(
+                out=bank[:],
+                lhsT=codes[:].bitcast(FP8X4),
+                lhsT_scale=scales[:],
+                rhs=key_words[j].bitcast(FP8X4),
+                rhs_scale=planes[4 * j : P, :],
+                start=True,
+                stop=True,
+            )
+            return bank
+
+        q2_codes, q2_scales = quantise(q2_raw, "q2")
+        q_codes, q_scales = quantise(q_raw, "q")
+        b_sb = sb.tile([P, T], F32, name="b_sb")
+        a_sb = sb.tile([P, T], F32, name="a_sb")
+        for j in range(PIECES):
+            bank = score(q2_codes, q2_scales, j, "b")
+            nc.scalar.copy(out=b_sb[:, j * PIECE : (j + 1) * PIECE], in_=bank[:])
+        a_banks = [score(q_codes, q_scales, j, "a") for j in range(PIECES)]
+
+        lam2 = sb.tile([P, 1], F32, name="lam2")
+        lam_neg = sb.tile([P, 1], F32, name="lam_neg")
+        nc.vector.tensor_scalar(lam2[:], lam_sb[:], 2.0, None, ALU.mult)
+        nc.vector.tensor_scalar(lam_neg[:], lam_sb[:], -1.0, None, ALU.mult)
+
+        def slots(lists, h):
+            return lists[:, h * HALF // GROUP : (h + 1) * HALF // GROUP]
+
+        sig = [sb.tile([P, HALF], F32, name=f"sig{h}") for h in range(HALVES)]
+        tl = [sb.tile([P, HALF], F32, name=f"tl{h}") for h in range(HALVES)]
+        first = [sb.tile([P, HALF], F32, name=f"first{h}") for h in range(HALVES)]
+        second = [sb.tile([P, HALF], F32, name=f"second{h}") for h in range(HALVES)]
+        picked = sb.tile([P, HALF], F32, name="picked")
+
+        def tanh_lam(h):
+            nc.vector.tensor_scalar(tl[h][:], sig[h][:], lam2[:], lam_neg[:], ALU.mult, ALU.add)
+
+        def put(h):
+            nc.vector.tensor_tensor(f1[:].indirect(slots(idx3, h)), first[h][:], second[h][:], ALU.add)
+
+        for h in range(HALVES):
+            nc.scalar.activation(sig[h][:], b_sb[:].indirect(slots(idx, h)), ACT.Sigmoid, scale=2.0)
+        for j in range(PIECES):
+            if j == PIECES - 1:
+                tanh_lam(0)
+            nc.vector.tensor_copy(out=a_sb[:, j * PIECE : (j + 1) * PIECE], in_=a_banks[j][:])
+
+        nc.scalar.activation(first[0][:], a_sb[:].indirect(slots(idx, 0)), ACT.Copy)
+        nc.scalar.activation(picked[:], a_sb[:].indirect(slots(idx2, 1)), ACT.Copy)
+        nc.scalar.activation(first[1][:], a_sb[:].indirect(slots(idx, 1)), ACT.Copy)
+        nc.vector.tensor_tensor(second[0][:], a_sb[:].indirect(slots(idx2, 0)), tl[0][:], ALU.mult)
+        tanh_lam(1)
+        put(0)
+        nc.vector.tensor_tensor(second[1][:], picked[:], tl[1][:], ALU.mult)
+        put(1)
+
+        larger = [sb.tile([P, PIECE], F32, name=f"larger{j}") for j in range(PIECES)]
+        result = [sb.tile([P, PIECE], F32, name=f"result{j}") for j in range(PIECES)]
+
+        def cols(j):
+            return slice(j * PIECE, (j + 1) * PIECE)
+
+        def take_larger(j):
+            nc.vector.tensor_tensor(larger[j][:], f1[:, cols(j)], old_sb[:, cols(j)], ALU.max)
+
+        def finish(j):
+            nc.vector.scalar_tensor_tensor(result[j][:], old_sb[:, cols(j)], 0.25, larger[j][:], ALU.mult, ALU.add)
+            nc.sync.dma_start(out=out[:, cols(j)], in_=result[j][:])
+
+        take_larger(0)
+        for j in range(1, PIECES):
+            take_larger(j)
+            finish(j - 1)
+        finish(PIECES - 1)

@@ -74,6 +74,10 @@ def tile_attend_turnedby_lean_largerput_heads_kernel(
         nc.sync.dma_start(idx3[:], offs3)
         nc.sync.dma_start(out=old_sb[:], in_=old)
 
+        warm = sb.tile([P, 1], F32, name="warm")
+        nc.vector.memset(warm[:], 0.0)
+        warm2 = sb.tile([P, 1], F32, name="warm2")
+        nc.scalar.activation(warm2[:], warm[:], ACT.Sigmoid)
         f1 = sb.tile([P, T], F32, name="f1")
         nc.vector.memset(f1[:], 0.0)
 

@@ -32,12 +32,12 @@ def tile_attend_turnedby_lean_largerput_heads_kernel(
         sb = ctx.enter_context(tc.tile_pool(name="sb", bufs=1))
         ps = ctx.enter_context(tc.psum_pool(name="ps", bufs=1))
 
-        planes = sb.tile([P, PIECE], U8, name="planes", align_bytes=64)
-        nc.vector.memset(planes[:].bitcast(I32), 0)
+        planes = sb.tile([P, T], U8, name="planes", align_bytes=64)
+        nc.gpsimd.memset(planes[:].bitcast(I32), 0)
 
         q2_raw = sb.tile([P, PACK, Q], F32, name="q2_raw")
         q_raw = sb.tile([P, PACK, Q], F32, name="q_raw")
-        key_loads = [(0, 2), (2, 3), (3, 4)]
+        key_loads = [(0, 3), (3, 4)]
         key_tiles = [
             sb.tile([P, (hi - lo) * PIECE], I32, name=f"key_words{lo}", align_bytes=64) for lo, hi in key_loads
         ]
@@ -55,21 +55,20 @@ def tile_attend_turnedby_lean_largerput_heads_kernel(
 
         nc.sync.dma_start(out=q2_raw[:], in_=query2.rearrange("(p j) m -> p j m", j=PACK))
         for quad in range(4):
-            nc.scalar.dma_start(
-                out=planes[32 * quad : 32 * quad + 16, :].bitcast(I32),
-                in_=scales_hbm[4 * quad : 4 * quad + 4, :].rearrange("r (j c) -> j r c", j=PIECES),
+            nc.sync.dma_start(
+                out=planes[32 * quad : 32 * quad + 4, :].bitcast(I32),
+                in_=scales_hbm[4 * quad : 4 * quad + 4, :],
             )
         load_keys(0)
         nc.sync.dma_start(out=q_raw[:], in_=query.rearrange("(p j) m -> p j m", j=PACK))
         load_keys(1)
-        load_keys(2)
         idx = sb.tile([P, I // GROUP], U16, name="idx")
         idx2 = sb.tile([P, I // GROUP], U16, name="idx2")
         idx3 = sb.tile([P, I // GROUP], U16, name="idx3")
         lam_sb = sb.tile([P, 1], F32, name="lam_sb")
         old_sb = sb.tile([P, T], F32, name="old_sb")
         nc.sync.dma_start(idx[:], offs)
-        nc.gpsimd.dma_start(out=lam_sb[:], in_=lam)
+        nc.sync.dma_start(out=lam_sb[:], in_=lam)
         nc.sync.dma_start(idx2[:], offs2)
         nc.sync.dma_start(idx3[:], offs3)
         nc.sync.dma_start(out=old_sb[:], in_=old)
@@ -101,7 +100,7 @@ def tile_attend_turnedby_lean_largerput_heads_kernel(
                 lhsT=codes[:].bitcast(FP8X4),
                 lhsT_scale=scales[:],
                 rhs=key_words[j].bitcast(FP8X4),
-                rhs_scale=planes[4 * j : P, :],
+                rhs_scale=planes[:, j * PIECE : (j + 1) * PIECE],
                 start=True,
                 stop=True,
             )
@@ -118,20 +117,20 @@ def tile_attend_turnedby_lean_largerput_heads_kernel(
 
         lam2 = sb.tile([P, 1], F32, name="lam2")
         lam_neg = sb.tile([P, 1], F32, name="lam_neg")
-        nc.vector.tensor_scalar(lam2[:], lam_sb[:], 2.0, None, ALU.mult)
-        nc.vector.tensor_scalar(lam_neg[:], lam_sb[:], -1.0, None, ALU.mult)
+        nc.gpsimd.tensor_scalar(lam2[:], lam_sb[:], 2.0, 0.0, ALU.mult, ALU.add)
+        nc.gpsimd.tensor_scalar(lam_neg[:], lam_sb[:], -1.0, 0.0, ALU.mult, ALU.add)
 
         def slots(lists, h):
             return lists[:, h * HALF // GROUP : (h + 1) * HALF // GROUP]
 
         sig = [sb.tile([P, HALF], F32, name=f"sig{h}") for h in range(HALVES)]
-        tl = [sb.tile([P, HALF], F32, name=f"tl{h}") for h in range(HALVES)]
+        tl = sb.tile([P, HALF], F32, name="tl")
         first = [sb.tile([P, HALF], F32, name=f"first{h}") for h in range(HALVES)]
         second = [sb.tile([P, HALF], F32, name=f"second{h}") for h in range(HALVES)]
         picked = sb.tile([P, HALF], F32, name="picked")
 
         def tanh_lam(h):
-            nc.vector.tensor_scalar(tl[h][:], sig[h][:], lam2[:], lam_neg[:], ALU.mult, ALU.add)
+            nc.vector.tensor_scalar(tl[:], sig[h][:], lam2[:], lam_neg[:], ALU.mult, ALU.add)
 
         def put(h):
             nc.vector.tensor_tensor(f1[:].indirect(slots(idx3, h)), first[h][:], second[h][:], ALU.add)
@@ -139,17 +138,16 @@ def tile_attend_turnedby_lean_largerput_heads_kernel(
         for h in range(HALVES):
             nc.scalar.activation(sig[h][:], b_sb[:].indirect(slots(idx, h)), ACT.Sigmoid, scale=2.0)
         for j in range(PIECES):
-            if j == PIECES - 1:
-                tanh_lam(0)
             nc.vector.tensor_copy(out=a_sb[:, j * PIECE : (j + 1) * PIECE], in_=a_banks[j][:])
 
+        tanh_lam(0)
         nc.scalar.activation(first[0][:], a_sb[:].indirect(slots(idx, 0)), ACT.Copy)
         nc.scalar.activation(picked[:], a_sb[:].indirect(slots(idx2, 1)), ACT.Copy)
         nc.scalar.activation(first[1][:], a_sb[:].indirect(slots(idx, 1)), ACT.Copy)
-        nc.vector.tensor_tensor(second[0][:], a_sb[:].indirect(slots(idx2, 0)), tl[0][:], ALU.mult)
+        nc.vector.tensor_tensor(second[0][:], a_sb[:].indirect(slots(idx2, 0)), tl[:], ALU.mult)
         tanh_lam(1)
         put(0)
-        nc.vector.tensor_tensor(second[1][:], picked[:], tl[1][:], ALU.mult)
+        nc.vector.tensor_tensor(second[1][:], picked[:], tl[:], ALU.mult)
         put(1)
 
         larger = [sb.tile([P, PIECE], F32, name=f"larger{j}") for j in range(PIECES)]

@@ -41,11 +41,13 @@ def tile_attend_turnedby_lean_largerput_heads_kernel(
         key_tiles = [
             sb.tile([P, (hi - lo) * PIECE], I32, name=f"key_words{lo}", align_bytes=64) for lo, hi in key_loads
         ]
-        key_words = [
-            key_tiles[n][:, (j - lo) * PIECE : (j - lo + 1) * PIECE]
-            for n, (lo, hi) in enumerate(key_loads)
-            for j in range(lo, hi)
-        ]
+        passes = [(0, 256), (256, 512), (512, 768), (768, 896), (896, 1024)]
+
+        def key_words(lo, hi):
+            n = 0 if lo < key_loads[1][0] * PIECE else 1
+            base = key_loads[n][0] * PIECE
+            return key_tiles[n][:, lo - base : hi - base]
+
         words_hbm = keys_words[0].rearrange("p n t -> p (n t)").bitcast(I32)
         scales_hbm = keys_scales[0].bitcast(I32)
 
@@ -54,12 +56,12 @@ def tile_attend_turnedby_lean_largerput_heads_kernel(
             nc.sync.dma_start(out=key_tiles[n][:], in_=words_hbm[:, lo * PIECE : hi * PIECE])
 
         nc.sync.dma_start(out=q2_raw[:], in_=query2.rearrange("(p j) m -> p j m", j=PACK))
+        load_keys(0)
         for quad in range(4):
             nc.sync.dma_start(
                 out=planes[32 * quad : 32 * quad + 4, :].bitcast(I32),
                 in_=scales_hbm[4 * quad : 4 * quad + 4, :],
             )
-        load_keys(0)
         nc.sync.dma_start(out=q_raw[:], in_=query.rearrange("(p j) m -> p j m", j=PACK))
         load_keys(1)
         idx = sb.tile([P, I // GROUP], U16, name="idx")
@@ -68,7 +70,7 @@ def tile_attend_turnedby_lean_largerput_heads_kernel(
         lam_sb = sb.tile([P, 1], F32, name="lam_sb")
         old_sb = sb.tile([P, T], F32, name="old_sb")
         nc.sync.dma_start(idx[:], offs)
-        nc.sync.dma_start(out=lam_sb[:], in_=lam)
+        nc.gpsimd.dma_start(out=lam_sb[:], in_=lam)
         nc.sync.dma_start(idx2[:], offs2)
         nc.sync.dma_start(idx3[:], offs3)
         nc.sync.dma_start(out=old_sb[:], in_=old)
@@ -93,14 +95,15 @@ def tile_attend_turnedby_lean_largerput_heads_kernel(
             )
             return codes, scales
 
-        def score(codes, scales, j, tag):
-            bank = ps.tile([P, PIECE], F32, name=f"{tag}_bank{j}")
+        def score(codes, scales, j, slot):
+            lo, hi = passes[j]
+            bank = ps.tile([P, hi - lo], F32, name=f"bank{slot}", tag=f"bank{slot % 8}")
             nc.tensor.matmul_mx(
                 out=bank[:],
                 lhsT=codes[:].bitcast(FP8X4),
                 lhsT_scale=scales[:],
-                rhs=key_words[j].bitcast(FP8X4),
-                rhs_scale=planes[:, j * PIECE : (j + 1) * PIECE],
+                rhs=key_words(lo, hi).bitcast(FP8X4),
+                rhs_scale=planes[:, lo:hi],
                 start=True,
                 stop=True,
             )
@@ -110,15 +113,16 @@ def tile_attend_turnedby_lean_largerput_heads_kernel(
         q_codes, q_scales = quantise(q_raw, "q")
         b_sb = sb.tile([P, T], F32, name="b_sb")
         a_sb = sb.tile([P, T], F32, name="a_sb")
-        for j in range(PIECES):
-            bank = score(q2_codes, q2_scales, j, "b")
-            nc.scalar.copy(out=b_sb[:, j * PIECE : (j + 1) * PIECE], in_=bank[:])
-        a_banks = [score(q_codes, q_scales, j, "a") for j in range(PIECES)]
+        for j, (lo, hi) in enumerate(passes):
+            bank = score(q2_codes, q2_scales, j, j)
+            if j < len(passes) - 1:
+                nc.scalar.copy(out=b_sb[:, lo:hi], in_=bank[:])
+            else:
+                nc.vector.tensor_copy(out=b_sb[:, lo:hi], in_=bank[:])
+        a_banks = [score(q_codes, q_scales, j, len(passes) + j) for j in range(len(passes))]
 
         lam2 = sb.tile([P, 1], F32, name="lam2")
-        lam_neg = sb.tile([P, 1], F32, name="lam_neg")
         nc.gpsimd.tensor_scalar(lam2[:], lam_sb[:], 2.0, 0.0, ALU.mult, ALU.add)
-        nc.gpsimd.tensor_scalar(lam_neg[:], lam_sb[:], -1.0, 0.0, ALU.mult, ALU.add)
 
         def slots(lists, h):
             return lists[:, h * HALF // GROUP : (h + 1) * HALF // GROUP]
@@ -130,15 +134,15 @@ def tile_attend_turnedby_lean_largerput_heads_kernel(
         picked = sb.tile([P, HALF], F32, name="picked")
 
         def tanh_lam(h):
-            nc.vector.tensor_scalar(tl[:], sig[h][:], lam2[:], lam_neg[:], ALU.mult, ALU.add)
+            nc.vector.tensor_scalar(tl[:], sig[h][:], -0.5, lam2[:], ALU.add, ALU.mult)
 
         def put(h):
             nc.vector.tensor_tensor(f1[:].indirect(slots(idx3, h)), first[h][:], second[h][:], ALU.add)
 
         for h in range(HALVES):
             nc.scalar.activation(sig[h][:], b_sb[:].indirect(slots(idx, h)), ACT.Sigmoid, scale=2.0)
-        for j in range(PIECES):
-            nc.vector.tensor_copy(out=a_sb[:, j * PIECE : (j + 1) * PIECE], in_=a_banks[j][:])
+        for (lo, hi), bank in zip(passes, a_banks):
+            nc.vector.tensor_copy(out=a_sb[:, lo:hi], in_=bank[:])
 
         tanh_lam(0)
         nc.scalar.activation(first[0][:], a_sb[:].indirect(slots(idx, 0)), ACT.Copy)
@@ -161,7 +165,8 @@ def tile_attend_turnedby_lean_largerput_heads_kernel(
 
         def finish(j):
             nc.vector.scalar_tensor_tensor(result[j][:], old_sb[:, cols(j)], 0.25, larger[j][:], ALU.mult, ALU.add)
-            nc.sync.dma_start(out=out[:, cols(j)], in_=result[j][:])
+            queue = nc.sync if j % 2 else nc.scalar
+            queue.dma_start(out=out[:, cols(j)], in_=result[j][:])
 
         take_larger(0)
         for j in range(1, PIECES):

from contextlib import ExitStack

import concourse.mybir as mybir

D, T, I, Q = 512, 1024, 512, 128
FLOPS = 2 * 2 * D * Q * T

F32 = mybir.dt.float32
BF16 = mybir.dt.bfloat16
I32 = mybir.dt.int32
U32 = mybir.dt.uint32
U16 = mybir.dt.uint16
U8 = mybir.dt.uint8
FP8X4 = mybir.dt.float8_e4m3fn_x4
ALU = mybir.AluOpType
ACT = mybir.ActivationFunctionType

P = 128
PACK = 4
PIECES = 4
PIECE = T // PIECES
HALVES = 2
HALF = I // HALVES
GROUP = 16


def tile_attend_turnedby_lean_largerput_heads_kernel(
    tc, query, query2, keys_words, keys_scales, lam, old, offs, offs2, offs3, out
):
    nc = tc.nc
    with ExitStack() as ctx:
        sb = ctx.enter_context(tc.tile_pool(name="sb", bufs=1))
        ps = ctx.enter_context(tc.psum_pool(name="ps", bufs=1))

        planes = sb.tile([P, T], U8, name="planes", align_bytes=64)
        nc.gpsimd.memset(planes[:].bitcast(I32), 0)

        q2_raw = sb.tile([P, PACK, Q], F32, name="q2_raw")
        q_raw = sb.tile([P, PACK, Q], F32, name="q_raw")
        key_loads = [(0, 3), (3, 4)]
        key_tiles = [
            sb.tile([P, (hi - lo) * PIECE], I32, name=f"key_words{lo}", align_bytes=64) for lo, hi in key_loads
        ]
        passes = [(0, 256), (256, 512), (512, 768), (768, 896), (896, 1024)]

        def key_words(lo, hi):
            n = 0 if lo < key_loads[1][0] * PIECE else 1
            base = key_loads[n][0] * PIECE
            return key_tiles[n][:, lo - base : hi - base]

        words_hbm = keys_words[0].rearrange("p n t -> p (n t)").bitcast(I32)
        scales_hbm = keys_scales[0].bitcast(I32)

        def load_keys(n):
            lo, hi = key_loads[n]
            nc.sync.dma_start(out=key_tiles[n][:], in_=words_hbm[:, lo * PIECE : hi * PIECE])

        nc.sync.dma_start(out=q2_raw[:], in_=query2.rearrange("(p j) m -> p j m", j=PACK))
        load_keys(0)
        for quad in range(4):
            nc.sync.dma_start(
                out=planes[32 * quad : 32 * quad + 4, :].bitcast(I32),
                in_=scales_hbm[4 * quad : 4 * quad + 4, :],
            )
        nc.sync.dma_start(out=q_raw[:], in_=query.rearrange("(p j) m -> p j m", j=PACK))
        load_keys(1)
        idx = sb.tile([P, I // GROUP], U16, name="idx")
        idx2 = sb.tile([P, I // GROUP], U16, name="idx2")
        idx3 = sb.tile([P, I // GROUP], U16, name="idx3")
        lam_sb = sb.tile([P, 1], F32, name="lam_sb")
        old_sb = sb.tile([P, T], F32, name="old_sb")
        nc.sync.dma_start(idx[:], offs)
        nc.gpsimd.dma_start(out=lam_sb[:], in_=lam)
        nc.sync.dma_start(idx2[:], offs2)
        nc.sync.dma_start(idx3[:], offs3)
        nc.sync.dma_start(out=old_sb[:], in_=old)

        warm = sb.tile([P, 1], F32, name="warm")
        nc.vector.memset(warm[:], 0.0)
        warm2 = sb.tile([P, 1], F32, name="warm2")
        nc.scalar.activation(warm2[:], warm[:], ACT.Sigmoid)
        f1 = sb.tile([P, T], F32, name="f1")
        nc.vector.memset(f1[:], 0.0)

        def quantise(raw, tag):
            grouped = sb.tile([P, Q, PACK], BF16, name=f"{tag}_grouped", align_bytes=64)
            nc.vector.tensor_copy(
                out=grouped[:].rearrange("p (c i) t -> p c t i", i=4),
                in_=raw[:].rearrange("p t (c i) -> p c t i", i=4),
            )
            codes = sb.tile([P, Q], U32, name=f"{tag}_codes", align_bytes=64)
            scales = sb.tile([P, Q], U8, name=f"{tag}_scales", align_bytes=64)
            nc.vector.quantize_mx(
                out=codes[:].bitcast(FP8X4), scales=scales[:], in_=grouped[:].rearrange("p m t -> p (m t)")
            )
            return codes, scales

        def score(codes, scales, j, slot):
            lo, hi = passes[j]
            bank = ps.tile([P, hi - lo], F32, name=f"bank{slot}", tag=f"bank{slot % 8}")
            nc.tensor.matmul_mx(
                out=bank[:],
                lhsT=codes[:].bitcast(FP8X4),
                lhsT_scale=scales[:],
                rhs=key_words(lo, hi).bitcast(FP8X4),
                rhs_scale=planes[:, lo:hi],
                start=True,
                stop=True,
            )
            return bank

        q2_codes, q2_scales = quantise(q2_raw, "q2")
        q_codes, q_scales = quantise(q_raw, "q")
        b_sb = sb.tile([P, T], F32, name="b_sb")
        a_sb = sb.tile([P, T], F32, name="a_sb")
        for j, (lo, hi) in enumerate(passes):
            bank = score(q2_codes, q2_scales, j, j)
            if j < len(passes) - 1:
                nc.scalar.copy(out=b_sb[:, lo:hi], in_=bank[:])
            else:
                nc.vector.tensor_copy(out=b_sb[:, lo:hi], in_=bank[:])
        a_banks = [score(q_codes, q_scales, j, len(passes) + j) for j in range(len(passes))]

        lam2 = sb.tile([P, 1], F32, name="lam2")
        nc.gpsimd.tensor_scalar(lam2[:], lam_sb[:], 2.0, 0.0, ALU.mult, ALU.add)

        def slots(lists, h):
            return lists[:, h * HALF // GROUP : (h + 1) * HALF // GROUP]

        sig = [sb.tile([P, HALF], F32, name=f"sig{h}") for h in range(HALVES)]
        tl = sb.tile([P, HALF], F32, name="tl")
        first = [sb.tile([P, HALF], F32, name=f"first{h}") for h in range(HALVES)]
        second = [sb.tile([P, HALF], F32, name=f"second{h}") for h in range(HALVES)]
        picked = sb.tile([P, HALF], F32, name="picked")

        def tanh_lam(h):
            nc.vector.tensor_scalar(tl[:], sig[h][:], -0.5, lam2[:], ALU.add, ALU.mult)

        def put(h):
            nc.vector.tensor_tensor(f1[:].indirect(slots(idx3, h)), first[h][:], second[h][:], ALU.add)

        for h in range(HALVES):
            nc.scalar.activation(sig[h][:], b_sb[:].indirect(slots(idx, h)), ACT.Sigmoid, scale=2.0)
        for (lo, hi), bank in zip(passes, a_banks):
            nc.vector.tensor_copy(out=a_sb[:, lo:hi], in_=bank[:])

        tanh_lam(0)
        nc.scalar.activation(first[0][:], a_sb[:].indirect(slots(idx, 0)), ACT.Copy)
        nc.scalar.activation(picked[:], a_sb[:].indirect(slots(idx2, 1)), ACT.Copy)
        nc.scalar.activation(first[1][:], a_sb[:].indirect(slots(idx, 1)), ACT.Copy)
        nc.vector.tensor_tensor(second[0][:], a_sb[:].indirect(slots(idx2, 0)), tl[:], ALU.mult)
        tanh_lam(1)
        put(0)
        nc.vector.tensor_tensor(second[1][:], picked[:], tl[:], ALU.mult)
        put(1)

        larger = [sb.tile([P, PIECE], F32, name=f"larger{j}") for j in range(PIECES)]
        result = [sb.tile([P, PIECE], F32, name=f"result{j}") for j in range(PIECES)]

        def cols(j):
            return slice(j * PIECE, (j + 1) * PIECE)

        def take_larger(j):
            nc.vector.tensor_tensor(larger[j][:], f1[:, cols(j)], old_sb[:, cols(j)], ALU.max)

        def finish(j):
            nc.vector.scalar_tensor_tensor(result[j][:], old_sb[:, cols(j)], 0.25, larger[j][:], ALU.mult, ALU.add)
            queue = nc.sync if j % 2 else nc.scalar
            queue.dma_start(out=out[:, cols(j)], in_=result[j][:])

        take_larger(0)
        for j in range(1, PIECES):
            take_larger(j)
            finish(j - 1)
        finish(PIECES - 1)
